import numpy as np
import ml_dtypes


def mxq(x, axis, fmt="e4m3"):
    dtype, down = {"e4m3": (ml_dtypes.float8_e4m3fn, 7), "e5m2": (ml_dtypes.float8_e5m2, 14)}[fmt]
    v = np.moveaxis(np.asarray(x, np.float32).astype(ml_dtypes.bfloat16).astype(np.float64), axis, -1)
    blocks = v.reshape(v.shape[:-1] + (-1, 32))
    amax = np.abs(blocks).max(-1, keepdims=True)
    byte = np.maximum(np.where(amax > 0, np.frexp(amax)[1] - 1 + 127, 0) - down, 1)
    scale = np.exp2(byte - 127.0)
    codes = (blocks / scale).astype(np.float32).astype(dtype).astype(np.float64)
    return np.moveaxis((codes * scale).reshape(v.shape), -1, axis)


WIDE = False


def mx_kscale(k):
    if not WIDE:
        return np.ones(k)
    levels = np.array([10, -10, 5, -5, 0])
    if k % 512:
        return np.exp2(np.random.permutation(np.resize(levels, k // 32))).repeat(32)
    a = np.empty((k // 512, 16))
    for p in range(k // 512):
        a[p, :8] = np.random.permutation(np.resize(levels, 8))
        for g in range(8):
            far = levels[np.abs(levels - a[p, g]) >= 10]
            a[p, g + 8] = far[np.random.randint(len(far))]
    return np.exp2(a.ravel()).repeat(32)


def f64(x):
    return np.asarray(x).astype(np.float64)


def striped(idx):
    return np.tile(idx.reshape(-1, 16).T, (8, 1)).astype(np.uint16)


def unstriped(offs):
    return offs[:16].T.reshape(-1).astype(np.int64)


def striped8(idx):
    return np.concatenate([x.reshape(-1, 16).T for x in idx]).astype(np.uint16)


def runs(offs, k):
    lists = np.stack([offs[16 * r : 16 * r + 16].T.reshape(-1) for r in range(8)]).astype(np.int64)
    return lists[np.arange(k) % 512 // 64]


def pack_weight(w):
    k, n = w.shape
    w = f64(np.asarray(w, np.float32).astype(ml_dtypes.bfloat16)).reshape(k // 32, 32, n)
    amax = np.abs(w).max(1)
    byte = np.clip(np.where(amax > 0, np.frexp(amax)[1] - 1 + 127 - 7, 1), 1, 254)
    scaled = (w * np.exp2(127.0 - byte)[:, None, :]).reshape(k, n).astype(np.float32)
    words = np.ascontiguousarray(scaled.reshape(k // 512, 128, 4, n).transpose(0, 1, 3, 2)).astype(ml_dtypes.float8_e4m3fn).view(np.uint8)
    return words, np.ascontiguousarray(byte.astype(np.uint8).reshape(k // 512, 16, n))


def unpack_weight(words, scales):
    g, p, n, _ = words.shape
    vals = np.ascontiguousarray(words).view(ml_dtypes.float8_e4m3fn).astype(np.float64) * np.repeat(np.exp2(scales.astype(np.float64) - 127.0), 8, axis=1)[..., None]
    return vals.transpose(0, 1, 3, 2).reshape(g * 512, n)

def planes(y):
    n, m = y.shape
    v = y.astype(np.float32).astype(ml_dtypes.bfloat16).astype(np.float64).reshape(n // 32, 32, m)
    top = np.abs(v).max(1)
    byte = np.clip(np.where(top > 0, np.frexp(top)[1] - 1 + 127 - 7, 1), 1, 254)
    codes = (v * np.exp2(127.0 - byte)[:, None, :]).reshape(n, m).astype(np.float32).astype(ml_dtypes.float8_e4m3fn).view(np.uint8)
    words = codes.reshape(n // 512, 128, 4, m).transpose(0, 1, 3, 2)
    return np.ascontiguousarray(words), np.ascontiguousarray(byte.astype(np.uint8).reshape(n // 512, 16, m))


K, T, S, N, H = 512, 2048, 512, 512, 512


def setup_inputs():
    n = np.random.standard_normal
    s = mx_kscale(K)[:, None]
    u = mx_kscale(H)
    packed_xT = pack_weight(n((K, T)) * s)
    packed_w1 = pack_weight(n((K, H)) / np.sqrt(K) / s)
    packed_w2 = pack_weight(n((H, H)) / np.sqrt(H) / u[:, None])
    packed_w3 = pack_weight(n((H, N)) / np.sqrt(H) / u[:, None])
    return {
        "x_words": packed_xT[0],
        "x_scales": packed_xT[1],
        "w1_words": packed_w1[0],
        "w1_scales": packed_w1[1],
        "gn": (np.random.uniform(0.5, 1.5, (H, 1)) * u[:, None]).astype(np.float32),
        "w2_words": packed_w2[0],
        "w2_scales": packed_w2[1],
        "res": n((N, S)).astype(np.float32),
        "w3_words": packed_w3[0],
        "w3_scales": packed_w3[1],
        "offs": striped(np.random.permutation(T)[:S]),
        "nx": striped8(np.random.randint(0, S, (8, S))),
        "mv": striped8(np.stack([np.random.permutation(S) for _ in range(8)])),
    }


def reference(x_words, x_scales, w1_words, w1_scales, gn, w2_words, w2_scales, res, w3_words, w3_scales, offs, nx, mv):
    xq = unpack_weight(x_words, x_scales)[:, unstriped(offs)]
    y = unpack_weight(w1_words, w1_scales).T @ xq
    p = y + y[np.arange(H)[:, None], runs(nx, H)]
    r2 = np.maximum(p, p[np.arange(H)[:, None], runs(nx, H)])
    z = f64(gn) * (r2 - (r2[np.arange(H)[:, None], runs(nx, H)]))
    h = np.tanh(unpack_weight(w2_words, w2_scales).T @ mxq(z, 0, "e4m3"))
    z2 = f64(gn) * (h[np.arange(H)[:, None], runs(mv, H)])
    out_0 = f64(res) + (unpack_weight(w3_words, w3_scales).T @ mxq(z2, 0, "e4m3"))
    return (out_0,) + planes(out_0)

@@ -1,0 +1,242 @@
+from contextlib import ExitStack
+
+import concourse.mybir as mybir
+
+K, T, S, N, H = 512, 2048, 512, 512, 512
+FLOPS = 2 * S * (K * H + H * H + H * N)
+
+F32 = mybir.dt.float32
+BF16 = mybir.dt.bfloat16
+I32 = mybir.dt.int32
+U32 = mybir.dt.uint32
+U16 = mybir.dt.uint16
+U8 = mybir.dt.uint8
+FP8X4 = mybir.dt.float8_e4m3fn_x4
+ALU = mybir.AluOpType
+ACT = mybir.ActivationFunctionType
+
+P = 128
+PACK = 4
+HALF = S // 2
+Z_CHUNKS = ((0, 256), (256, 128), (384, 128))
+OUT_CHUNKS = ((0, 128), (128, 128), (256, 128), (384, 128))
+
+
+def words_view(words):
+    return words[0].rearrange("p c r -> p (c r)").bitcast(I32)
+
+
+def load_scale_rows(queue, tile, scales, first_row):
+    for q in range(4):
+        queue.dma_start(
+            out=tile[32 * q + first_row : 32 * q + first_row + 4, :].bitcast(I32),
+            in_=scales[0, 4 * q : 4 * q + 4, :].bitcast(I32),
+        )
+
+
+def deal(engine, dealt, raw):
+    engine.tensor_copy(
+        out=dealt.rearrange("p (t m) -> p t m", t=PACK),
+        in_=raw.rearrange("p (m t) -> p t m", t=PACK),
+    )
+
+
+def interleave(copy, grouped, planes):
+    copy(
+        out=grouped.rearrange("p (c i) t -> p c t i", i=4),
+        in_=planes.rearrange("p t (c i) -> p c t i", i=4),
+    )
+
+
+def offsets(lists, first, width):
+    return lists[:, first // 16 : (first + width) // 16]
+
+
+def tile_picked_alldbl3_none_po_kernel(
+    tc, x_words, x_scales, w1_words, w1_scales, gn, w2_words, w2_scales, res, w3_words, w3_scales,
+    offs, nx, mv, out_0, out_1, out_2,
+):
+    nc = tc.nc
+    with ExitStack() as ctx:
+        sb = ctx.enter_context(tc.tile_pool(name="sb", bufs=1))
+        psum = ctx.enter_context(tc.psum_pool(name="psum", bufs=1))
+
+        def sbuf(name, shape, dtype):
+            return sb.tile(shape, dtype, name=name, align_bytes=64)
+
+        def bank(number, name, shape):
+            return psum.tile(shape, F32, name=name, tag="bank%d" % number)
+
+        offs_sb = sbuf("offs_sb", [P, S // 16], U16)
+        nx_sb = sbuf("nx_sb", [P, S // 16], U16)
+        mv_sb = sbuf("mv_sb", [P, S // 16], U16)
+        x_table = sbuf("x_table", [P, T], I32)
+        x_scale_table = sbuf("x_scale_table", [P, T], U8)
+        w_raw = [sbuf("w_raw%d" % i, [P, H], I32) for i in range(3)]
+        w_codes = [sbuf("w_codes%d" % i, [P, H], I32) for i in range(3)]
+        w1_scale_raw = sbuf("w1_scale_raw", [P, H], U8)
+        w23_scale_raw = sbuf("w23_scale_raw", [P, H], U8)
+        w1_scale = sbuf("w1_scale", [P, H], U8)
+        w23_scale = sbuf("w23_scale", [P, H], U8)
+        gain = sbuf("gain", [P, PACK], F32)
+        neg_gain = sbuf("neg_gain", [P, PACK], F32)
+        res_sb = sbuf("res_sb", [P, PACK, S], F32)
+
+        nc.gpsimd.memset(x_scale_table[:].bitcast(I32), 0)
+        nc.gpsimd.memset(w1_scale_raw[:].bitcast(I32), 0)
+        nc.gpsimd.memset(w23_scale_raw[:].bitcast(I32), 0)
+
+        nc.sync.dma_start(offs_sb[:], offs)
+        nc.sync.dma_start(out=w_raw[0][:], in_=words_view(w1_words))
+        nc.sync.dma_start(out=x_table[:], in_=words_view(x_words))
+        load_scale_rows(nc.scalar, x_scale_table, x_scales, 0)
+        load_scale_rows(nc.scalar, w1_scale_raw, w1_scales, 0)
+        nc.sync.dma_start(nx_sb[:], nx)
+        nc.sync.dma_start(out=gain[:], in_=gn.rearrange("(p t) o -> p (t o)", t=PACK))
+        nc.sync.dma_start(out=w_raw[1][:], in_=words_view(w2_words))
+        nc.sync.dma_start(out=w_raw[2][:], in_=words_view(w3_words))
+        load_scale_rows(nc.sync, w23_scale_raw, w2_scales, 0)
+        load_scale_rows(nc.sync, w23_scale_raw, w3_scales, 4)
+        nc.sync.dma_start(mv_sb[:], mv)
+        nc.sync.dma_start(out=res_sb[:], in_=res.rearrange("(p t) n -> p t n", t=PACK))
+
+        x_scale = sbuf("x_scale", [P, S], U8)
+        x_codes = sbuf("x_codes", [P, S], U32)
+        deal(nc.vector, w_codes[0][:], w_raw[0][:])
+        nc.vector.tensor_copy(x_scale[:], x_scale_table[:].indirect(offs_sb[:]))
+        deal(nc.vector, w1_scale[:], w1_scale_raw[:])
+        for half in range(2):
+            nc.vector.tensor_copy(
+                x_codes[:, half * HALF : (half + 1) * HALF],
+                x_table[:].bitcast(U32).indirect(offsets(offs_sb, half * HALF, HALF)),
+            )
+        y = [sbuf("y%d" % t, [P, S], F32) for t in range(PACK)]
+        y_twin = [sbuf("y_twin%d" % t, [P, S], F32) for t in range(PACK)]
+        for t in range(PACK):
+            pieces = ((0, HALF), (HALF, HALF)) if t == 0 else ((0, S),)
+            accs = []
+            for first, width in pieces:
+                cols = slice(first, first + width)
+                acc = bank(2 * t + first // HALF, "y_acc%d_%d" % (t, first), [P, width])
+                nc.tensor.matmul_mx(
+                    out=acc[:],
+                    lhsT=w_codes[0][:, t * P : (t + 1) * P].bitcast(FP8X4),
+                    lhsT_scale=w1_scale[:, t * P : (t + 1) * P],
+                    rhs=x_codes[:, cols].bitcast(FP8X4),
+                    rhs_scale=x_scale[:, cols],
+                    start=True,
+                    stop=True,
+                )
+                nc.scalar.copy(out=y_twin[t][:, cols], in_=acc[:])
+                nc.scalar.copy(out=y[t][:, cols], in_=acc[:])
+
+        nc.scalar.activation(out=neg_gain[:], in_=gain[:], func=ACT.Copy, scale=-1.0)
+
+        p = [sbuf("p%d" % t, [P, S], F32) for t in range(PACK)]
+        for t in range(PACK):
+            for half in range(2):
+                cols = slice(half * HALF, (half + 1) * HALF)
+                nc.vector.tensor_tensor(
+                    p[t][:, cols], y[t][:].indirect(offsets(nx_sb, half * HALF, HALF)), y_twin[t][:, cols], ALU.add
+                )
+
+        p_next = [sbuf("p_next%d" % t, [P, S], F32) for t in range(PACK)]
+        r2 = [sbuf("r2_%d" % t, [P, S], F32) for t in range(PACK)]
+        r2_gain = [sbuf("r2_gain%d" % t, [P, S], F32) for t in range(PACK)]
+        r2_twin = [sbuf("r2_twin%d" % t, [P, S], F32) for t in range(PACK)]
+
+        def larger(t):
+            nc.vector.tensor_tensor(r2[t][:], p[t][:], p_next[t][:], ALU.max)
+            nc.scalar.activation(out=r2_gain[t][:], in_=r2[t][:], func=ACT.Copy, scale=neg_gain[:, t : t + 1])
+            nc.scalar.activation(out=r2_twin[t][:], in_=r2[t][:], func=ACT.Copy, scale=neg_gain[:, t : t + 1])
+
+        for t in range(PACK):
+            for half in range(2):
+                cols = slice(half * HALF, (half + 1) * HALF)
+                nc.vector.tensor_copy(p_next[t][:, cols], p[t][:].indirect(offsets(nx_sb, half * HALF, HALF)))
+            if t > 0:
+                larger(t - 1)
+        larger(PACK - 1)
+
+        deal(nc.vector, w_codes[1][:], w_raw[1][:])
+        deal(nc.vector, w23_scale[:], w23_scale_raw[:])
+        deal(nc.vector, w_codes[2][:], w_raw[2][:])
+
+        h_acc = [[bank(2 * t + half, "h_acc%d_%d" % (t, half), [P, HALF]) for half in range(2)] for t in range(PACK)]
+        for c, (first, width) in enumerate(Z_CHUNKS):
+            cols = slice(first, first + width)
+            z = sbuf("z%d" % c, [P, PACK, width], F32)
+            for t in range(PACK):
+                nc.vector.tensor_tensor(
+                    z[:, t, :], r2_gain[t][:].indirect(offsets(nx_sb, first, width)), r2_twin[t][:, cols], ALU.subtract
+                )
+            z_grouped = sbuf("z_grouped%d" % c, [P, width, PACK], BF16)
+            interleave(nc.vector.tensor_copy if c == len(Z_CHUNKS) - 1 else nc.scalar.copy, z_grouped[:], z[:])
+            z_codes = sbuf("z_codes%d" % c, [P, width], U32)
+            z_scale = sbuf("z_scale%d" % c, [P, width], U8)
+            nc.vector.quantize_mx(
+                out=z_codes[:].bitcast(FP8X4), scales=z_scale[:], in_=z_grouped[:].rearrange("p c t -> p (c t)")
+            )
+            for t in range(PACK):
+                nc.tensor.matmul_mx(
+                    out=h_acc[t][first // HALF][:, first % HALF : first % HALF + width],
+                    lhsT=w_codes[1][:, t * P : (t + 1) * P].bitcast(FP8X4),
+                    lhsT_scale=w23_scale[:, t * P : (t + 1) * P],
+                    rhs=z_codes[:].bitcast(FP8X4),
+                    rhs_scale=z_scale[:],
+                    start=True,
+                    stop=True,
+                )
+
+        h = [sbuf("h%d" % t, [P, S], F32) for t in range(PACK)]
+        h_gain = [sbuf("h_gain%d" % t, [P, S], F32) for t in range(PACK)]
+        for t in range(PACK):
+            for half in range(2):
+                cols = slice(half * HALF, (half + 1) * HALF)
+                nc.scalar.activation(out=h[t][:, cols], in_=h_acc[t][half][:], func=ACT.Tanh)
+            nc.vector.tensor_scalar(h_gain[t][:], h[t][:], gain[:, t : t + 1], None, ALU.mult)
+
+        out_rows = out_0.rearrange("(p t) n -> p t n", t=PACK)
+        out_scale = sbuf("out_scale", [P, S], U8)
+        for c, (first, width) in enumerate(OUT_CHUNKS):
+            cols = slice(first, first + width)
+            last = c == len(OUT_CHUNKS) - 1
+            z2 = sbuf("z2_%d" % c, [P, PACK, width], F32)
+            for t in range(PACK):
+                nc.vector.tensor_copy(z2[:, t, :], h_gain[t][:].indirect(offsets(mv_sb, first, width)))
+            z2_grouped = sbuf("z2_grouped%d" % c, [P, width, PACK], BF16)
+            interleave(nc.scalar.copy, z2_grouped[:], z2[:])
+            z2_codes = sbuf("z2_codes%d" % c, [P, width], U32)
+            z2_scale = sbuf("z2_scale%d" % c, [P, width], U8)
+            nc.vector.quantize_mx(
+                out=z2_codes[:].bitcast(FP8X4), scales=z2_scale[:], in_=z2_grouped[:].rearrange("p c t -> p (c t)")
+            )
+            acc = bank(c, "out_acc%d" % c, [P, PACK, width])
+            for t in range(PACK):
+                nc.tensor.matmul_mx(
+                    out=acc[:, t, :],
+                    lhsT=w_codes[2][:, t * P : (t + 1) * P].bitcast(FP8X4),
+                    lhsT_scale=w23_scale[4:P, t * P : (t + 1) * P],
+                    rhs=z2_codes[:].bitcast(FP8X4),
+                    rhs_scale=z2_scale[:],
+                    start=True,
+                    stop=True,
+                )
+            result = sbuf("result%d" % c, [P, PACK, width], F32)
+            nc.vector.tensor_tensor(result[:], acc[:], res_sb[:, :, cols], ALU.add)
+            nc.sync.dma_start(out=out_rows[:, :, cols], in_=result[:])
+            out_grouped = sbuf("out_grouped%d" % c, [P, width, PACK], BF16)
+            interleave(nc.vector.tensor_copy if last else nc.scalar.copy, out_grouped[:], result[:])
+            out_codes = sbuf("out_codes%d" % c, [P, width], I32)
+            nc.vector.quantize_mx(
+                out=out_codes[:].bitcast(FP8X4),
+                scales=out_scale[:, cols],
+                in_=out_grouped[:].rearrange("p c t -> p (c t)"),
+            )
+            nc.sync.dma_start(out=words_view(out_1)[:, cols], in_=out_codes[:])
+        for q in range(4):
+            queue = nc.scalar if q % 2 else nc.sync
+            queue.dma_start(
+                out=out_2[0, 4 * q : 4 * q + 4, :].bitcast(I32),
+                in_=out_scale[32 * q : 32 * q + 4, :].bitcast(I32),
+            )

@@ -18,26 +18,25 @@ ACT = mybir.ActivationFunctionType
 P = 128
 PACK = 4
 HALF = S // 2
-Z_CHUNKS = ((0, 256), (256, 128), (384, 128))
-OUT_CHUNKS = ((0, 128), (128, 128), (256, 128), (384, 128))
+SPLIT = 160
 
 
 def words_view(words):
     return words[0].rearrange("p c r -> p (c r)").bitcast(I32)
 
 
-def load_scale_rows(queue, tile, scales, first_row):
+def load_scale_rows(queues, tile, scales, first_row):
     for q in range(4):
-        queue.dma_start(
+        queues[q].dma_start(
             out=tile[32 * q + first_row : 32 * q + first_row + 4, :].bitcast(I32),
             in_=scales[0, 4 * q : 4 * q + 4, :].bitcast(I32),
         )
 
 
-def deal(engine, dealt, raw):
+def deal(engine, dealt, raw, first, end):
     engine.tensor_copy(
-        out=dealt.rearrange("p (t m) -> p t m", t=PACK),
-        in_=raw.rearrange("p (m t) -> p t m", t=PACK),
+        out=dealt[:].rearrange("p (t m) -> p t m", t=PACK)[:, first:end, :],
+        in_=raw[:].rearrange("p (m t) -> p t m", t=PACK)[:, first:end, :],
     )
 
 
@@ -61,8 +60,8 @@ def tile_picked_alldbl3_none_po_kernel(
         sb = ctx.enter_context(tc.tile_pool(name="sb", bufs=1))
         psum = ctx.enter_context(tc.psum_pool(name="psum", bufs=1))
 
-        def sbuf(name, shape, dtype):
-            return sb.tile(shape, dtype, name=name, align_bytes=64)
+        def sbuf(name, shape, dtype, tag=""):
+            return sb.tile(shape, dtype, name=name, align_bytes=64, tag=tag or name)
 
         def bank(number, name, shape):
             return psum.tile(shape, F32, name=name, tag="bank%d" % number)
@@ -70,164 +69,202 @@ def tile_picked_alldbl3_none_po_kernel(
         offs_sb = sbuf("offs_sb", [P, S // 16], U16)
         nx_sb = sbuf("nx_sb", [P, S // 16], U16)
         mv_sb = sbuf("mv_sb", [P, S // 16], U16)
-        x_table = sbuf("x_table", [P, T], I32)
-        x_scale_table = sbuf("x_scale_table", [P, T], U8)
-        w_raw = [sbuf("w_raw%d" % i, [P, H], I32) for i in range(3)]
-        w_codes = [sbuf("w_codes%d" % i, [P, H], I32) for i in range(3)]
-        w1_scale_raw = sbuf("w1_scale_raw", [P, H], U8)
-        w23_scale_raw = sbuf("w23_scale_raw", [P, H], U8)
+        x_table = sbuf("x_table", [P, T], I32, "big_load")
+        x_scale_table = sbuf("x_scale_table", [P, T], U8, "scale_table")
+        w1_raw = sbuf("w1_raw", [P, H], I32, "w_load")
+        w1_codes = sbuf("w1_codes", [P, H], I32)
+        w1_scale_raw = sbuf("w1_scale_raw", [P, H], U8, "scale_load")
         w1_scale = sbuf("w1_scale", [P, H], U8)
-        w23_scale = sbuf("w23_scale", [P, H], U8)
         gain = sbuf("gain", [P, PACK], F32)
-        neg_gain = sbuf("neg_gain", [P, PACK], F32)
-        res_sb = sbuf("res_sb", [P, PACK, S], F32)
-
-        nc.gpsimd.memset(x_scale_table[:].bitcast(I32), 0)
-        nc.gpsimd.memset(w1_scale_raw[:].bitcast(I32), 0)
-        nc.gpsimd.memset(w23_scale_raw[:].bitcast(I32), 0)
 
         nc.sync.dma_start(offs_sb[:], offs)
-        nc.sync.dma_start(out=w_raw[0][:], in_=words_view(w1_words))
-        nc.sync.dma_start(out=x_table[:], in_=words_view(x_words))
-        load_scale_rows(nc.scalar, x_scale_table, x_scales, 0)
-        load_scale_rows(nc.scalar, w1_scale_raw, w1_scales, 0)
         nc.sync.dma_start(nx_sb[:], nx)
-        nc.sync.dma_start(out=gain[:], in_=gn.rearrange("(p t) o -> p (t o)", t=PACK))
-        nc.sync.dma_start(out=w_raw[1][:], in_=words_view(w2_words))
-        nc.sync.dma_start(out=w_raw[2][:], in_=words_view(w3_words))
-        load_scale_rows(nc.sync, w23_scale_raw, w2_scales, 0)
-        load_scale_rows(nc.sync, w23_scale_raw, w3_scales, 4)
         nc.sync.dma_start(mv_sb[:], mv)
-        nc.sync.dma_start(out=res_sb[:], in_=res.rearrange("(p t) n -> p t n", t=PACK))
+        nc.sync.dma_start(out=w1_raw[:], in_=words_view(w1_words))
+        nc.sync.dma_start(out=x_table[:], in_=words_view(x_words))
+        nc.gpsimd.memset(w1_scale_raw[:].bitcast(I32), 0)
+        load_scale_rows([nc.scalar] * 4, w1_scale_raw, w1_scales, 0)
+        nc.gpsimd.memset(x_scale_table[:].bitcast(I32), 0)
+        load_scale_rows([nc.scalar] * 4, x_scale_table, x_scales, 0)
+        nc.gpsimd.dma_start(out=gain[:], in_=gn.rearrange("(p t) o -> p (t o)", t=PACK))
 
-        x_scale = sbuf("x_scale", [P, S], U8)
-        x_codes = sbuf("x_codes", [P, S], U32)
-        deal(nc.vector, w_codes[0][:], w_raw[0][:])
-        nc.vector.tensor_copy(x_scale[:], x_scale_table[:].indirect(offs_sb[:]))
-        deal(nc.vector, w1_scale[:], w1_scale_raw[:])
+        gain_rows = sbuf("gain_rows", [P, PACK - 1, HALF], F32)
+        nc.gpsimd.tensor_copy(gain_rows[:], gain[:, : PACK - 1].unsqueeze(2).to_broadcast([P, PACK - 1, HALF]))
+        gain_last = sbuf("gain_last", [P, HALF], F32)
+        nc.gpsimd.tensor_copy(gain_last[:], gain[:, PACK - 2 : PACK - 1].to_broadcast([P, HALF]))
+        affine = sbuf("affine", [P, 2], F32)
+        nc.gpsimd.tensor_scalar(affine[:, 0:1], gain[:, PACK - 1 :], 2.0, 0.0, ALU.mult, ALU.add)
+        nc.gpsimd.tensor_scalar(affine[:, 1:2], gain[:, PACK - 1 :], -1.0, 0.0, ALU.mult, ALU.add)
+
+        x_scale = sbuf("x_scale", [P, S], U8, "picked_scale")
+        x_codes = sbuf("x_codes", [P, S], U32, "picked_codes")
+        deal(nc.vector, w1_codes, w1_raw, 0, PACK)
+        nc.vector.tensor_copy(x_codes[:], x_table[:].bitcast(U32).indirect(offs_sb[:]))
+        deal(nc.vector, w1_scale, w1_scale_raw, 0, PACK)
         for half in range(2):
             nc.vector.tensor_copy(
-                x_codes[:, half * HALF : (half + 1) * HALF],
-                x_table[:].bitcast(U32).indirect(offsets(offs_sb, half * HALF, HALF)),
+                x_scale[:, half * HALF : (half + 1) * HALF],
+                x_scale_table[:].indirect(offsets(offs_sb, half * HALF, HALF)),
             )
-        y = [sbuf("y%d" % t, [P, S], F32) for t in range(PACK)]
-        y_twin = [sbuf("y_twin%d" % t, [P, S], F32) for t in range(PACK)]
+        w2_raw = sbuf("w2_raw", [P, H], I32, "w_load")
+        nc.sync.dma_start(out=w2_raw[:], in_=words_view(w2_words))
+        w2_codes = sbuf("w2_codes", [P, H], I32, "scale_table")
+        deal(nc.vector, w2_codes, w2_raw, 0, PACK)
+        w23_scale_raw = sbuf("w23_scale_raw", [P, H], U8, "scale_load")
+        nc.gpsimd.memset(w23_scale_raw[:].bitcast(I32), 0)
+        load_scale_rows([nc.sync] * 4, w23_scale_raw, w2_scales, 0)
+        load_scale_rows([nc.sync] * 4, w23_scale_raw, w3_scales, 4)
+        res_sb = sbuf("res_sb", [P, PACK, S], F32, "big_load")
+        nc.sync.dma_start(out=res_sb[:], in_=res.rearrange("(p t) n -> p t n", t=PACK))
+
+        halves = ((0, HALF), (HALF, HALF))
+
+        def windows_and_twins(name):
+            wins = [sbuf("%s_win%d" % (name, t), [P, S if t == 0 else 2 * S], F32) for t in range(PACK)]
+            last_twin = sbuf("%s_last_twin" % name, [P, S], F32, "%s_twin" % name)
+            return wins, [wins[t + 1][:, S:] for t in range(PACK - 1)] + [last_twin[:]]
+
+        y_win, y_twin = windows_and_twins("y")
+        p_win, p_twin = windows_and_twins("p")
         for t in range(PACK):
-            pieces = ((0, HALF), (HALF, HALF)) if t == 0 else ((0, S),)
-            accs = []
+            pieces = halves if t == 0 else ((0, S),)
             for first, width in pieces:
                 cols = slice(first, first + width)
                 acc = bank(2 * t + first // HALF, "y_acc%d_%d" % (t, first), [P, width])
                 nc.tensor.matmul_mx(
                     out=acc[:],
-                    lhsT=w_codes[0][:, t * P : (t + 1) * P].bitcast(FP8X4),
+                    lhsT=w1_codes[:, t * P : (t + 1) * P].bitcast(FP8X4),
                     lhsT_scale=w1_scale[:, t * P : (t + 1) * P],
                     rhs=x_codes[:, cols].bitcast(FP8X4),
                     rhs_scale=x_scale[:, cols],
                     start=True,
                     stop=True,
                 )
+                nc.scalar.copy(out=y_win[t][:, cols], in_=acc[:])
                 nc.scalar.copy(out=y_twin[t][:, cols], in_=acc[:])
-                nc.scalar.copy(out=y[t][:, cols], in_=acc[:])
-
-        nc.scalar.activation(out=neg_gain[:], in_=gain[:], func=ACT.Copy, scale=-1.0)
-
-        p = [sbuf("p%d" % t, [P, S], F32) for t in range(PACK)]
-        for t in range(PACK):
-            for half in range(2):
-                cols = slice(half * HALF, (half + 1) * HALF)
+            for first, width in pieces:
+                cols = slice(first, first + width)
                 nc.vector.tensor_tensor(
-                    p[t][:, cols], y[t][:].indirect(offsets(nx_sb, half * HALF, HALF)), y_twin[t][:, cols], ALU.add
+                    p_win[t][:, cols], y_win[t][:].indirect(offsets(nx_sb, first, width)), y_twin[t][:, cols], ALU.add
+                )
+        for t in range(PACK):
+            nc.scalar.copy(out=p_twin[t], in_=p_win[t][:, :S])
+
+        w23_scale = sbuf("w23_scale", [P, H], U8, "y_twin")
+        deal(nc.vector, w23_scale, w23_scale_raw, 0, PACK)
+        step = [sbuf("step%d" % t, [P, S], F32) for t in range(PACK)]
+        rise = [sbuf("rise%d" % t, [P, S], F32) for t in range(PACK)]
+        fall = [[sbuf("fall%d_%d" % (t, half), [P, HALF], F32) for half in range(2)] for t in range(PACK)]
+        for t in range(PACK):
+            for first, width in halves if t == 0 else ((0, S),):
+                cols = slice(first, first + width)
+                nc.vector.tensor_tensor(
+                    step[t][:, cols],
+                    p_win[t][:].indirect(offsets(nx_sb, first, width)),
+                    p_twin[t][:, cols],
+                    ALU.subtract,
+                )
+            nc.scalar.activation(out=rise[t][:], in_=step[t][:], func=ACT.Relu)
+            for half, (first, width) in enumerate(halves):
+                nc.scalar.activation(
+                    out=fall[t][half][:], in_=step[t][:, first : first + width], func=ACT.Relu, scale=-1.0
                 )
 
-        p_next = [sbuf("p_next%d" % t, [P, S], F32) for t in range(PACK)]
-        r2 = [sbuf("r2_%d" % t, [P, S], F32) for t in range(PACK)]
-        r2_gain = [sbuf("r2_gain%d" % t, [P, S], F32) for t in range(PACK)]
-        r2_twin = [sbuf("r2_twin%d" % t, [P, S], F32) for t in range(PACK)]
-
-        def larger(t):
-            nc.vector.tensor_tensor(r2[t][:], p[t][:], p_next[t][:], ALU.max)
-            nc.scalar.activation(out=r2_gain[t][:], in_=r2[t][:], func=ACT.Copy, scale=neg_gain[:, t : t + 1])
-            nc.scalar.activation(out=r2_twin[t][:], in_=r2[t][:], func=ACT.Copy, scale=neg_gain[:, t : t + 1])
-
-        for t in range(PACK):
-            for half in range(2):
-                cols = slice(half * HALF, (half + 1) * HALF)
-                nc.vector.tensor_copy(p_next[t][:, cols], p[t][:].indirect(offsets(nx_sb, half * HALF, HALF)))
-            if t > 0:
-                larger(t - 1)
-        larger(PACK - 1)
-
-        deal(nc.vector, w_codes[1][:], w_raw[1][:])
-        deal(nc.vector, w23_scale[:], w23_scale_raw[:])
-        deal(nc.vector, w_codes[2][:], w_raw[2][:])
+        def quantise(name, grouped):
+            codes = sbuf(name + "_codes", [P, HALF], U32)
+            scale = sbuf(name + "_scale", [P, HALF], U8)
+            nc.vector.quantize_mx(
+                out=codes[:].bitcast(FP8X4), scales=scale[:], in_=grouped[:].rearrange("p c t -> p (c t)")
+            )
+            return codes, scale
 
         h_acc = [[bank(2 * t + half, "h_acc%d_%d" % (t, half), [P, HALF]) for half in range(2)] for t in range(PACK)]
-        for c, (first, width) in enumerate(Z_CHUNKS):
-            cols = slice(first, first + width)
-            z = sbuf("z%d" % c, [P, PACK, width], F32)
+        h = [sbuf("h%d" % t, [P, S], F32) for t in range(PACK)]
+        for half, (first, width) in enumerate(halves):
+            diff = sbuf("diff%d" % half, [P, PACK, HALF], F32, "fall3_0" if half else "p_win3")
+            z_grouped = sbuf("z_grouped%d" % half, [P, HALF, PACK], BF16, "z_grouped")
             for t in range(PACK):
                 nc.vector.tensor_tensor(
-                    z[:, t, :], r2_gain[t][:].indirect(offsets(nx_sb, first, width)), r2_twin[t][:, cols], ALU.subtract
+                    diff[:, t, :], rise[t][:].indirect(offsets(nx_sb, first, width)), fall[t][half][:], ALU.subtract
                 )
-            z_grouped = sbuf("z_grouped%d" % c, [P, width, PACK], BF16)
-            interleave(nc.vector.tensor_copy if c == len(Z_CHUNKS) - 1 else nc.scalar.copy, z_grouped[:], z[:])
-            z_codes = sbuf("z_codes%d" % c, [P, width], U32)
-            z_scale = sbuf("z_scale%d" % c, [P, width], U8)
-            nc.vector.quantize_mx(
-                out=z_codes[:].bitcast(FP8X4), scales=z_scale[:], in_=z_grouped[:].rearrange("p c t -> p (c t)")
-            )
+            if half == 0:
+                z = sbuf("z", [P, PACK, HALF], F32)
+                for t in range(PACK):
+                    nc.scalar.activation(out=z[:, t, :], in_=diff[:, t, :], func=ACT.Copy, scale=gain[:, t : t + 1])
+                interleave(nc.scalar.copy, z_grouped[:], z[:])
+            else:
+                nc.vector.tensor_tensor(
+                    z_grouped[:].rearrange("p (c i) t -> p c t i", i=4),
+                    diff[:].rearrange("p t (c i) -> p c t i", i=4),
+                    gain[:].unsqueeze(1).unsqueeze(3).to_broadcast([P, HALF // 4, PACK, 4]),
+                    ALU.mult,
+                )
+            z_codes, z_scale = quantise("z%d" % half, z_grouped)
             for t in range(PACK):
                 nc.tensor.matmul_mx(
-                    out=h_acc[t][first // HALF][:, first % HALF : first % HALF + width],
-                    lhsT=w_codes[1][:, t * P : (t + 1) * P].bitcast(FP8X4),
+                    out=h_acc[t][half][:],
+                    lhsT=w2_codes[:, t * P : (t + 1) * P].bitcast(FP8X4),
                     lhsT_scale=w23_scale[:, t * P : (t + 1) * P],
                     rhs=z_codes[:].bitcast(FP8X4),
                     rhs_scale=z_scale[:],
                     start=True,
                     stop=True,
                 )
-
-        h = [sbuf("h%d" % t, [P, S], F32) for t in range(PACK)]
-        h_gain = [sbuf("h_gain%d" % t, [P, S], F32) for t in range(PACK)]
+        w3_raw = sbuf("w3_raw", [P, H], I32, "w_load")
+        nc.sync.dma_start(out=w3_raw[:], in_=words_view(w3_words))
+        w3_codes = sbuf("w3_codes", [P, H], I32, "p_twin")
+        deal(nc.vector, w3_codes, w3_raw, 0, PACK)
         for t in range(PACK):
-            for half in range(2):
-                cols = slice(half * HALF, (half + 1) * HALF)
-                nc.scalar.activation(out=h[t][:, cols], in_=h_acc[t][half][:], func=ACT.Tanh)
-            nc.vector.tensor_scalar(h_gain[t][:], h[t][:], gain[:, t : t + 1], None, ALU.mult)
+            for half, (first, width) in enumerate(halves):
+                if t < PACK - 1:
+                    nc.scalar.activation(
+                        out=h[t][:, first : first + width], in_=h_acc[t][half][:], func=ACT.Tanh, scale=-1.0
+                    )
+                else:
+                    nc.scalar.activation(
+                        out=h[t][:, first : first + width], in_=h_acc[t][half][:], func=ACT.Copy, scale=-2.0
+                    )
 
         out_rows = out_0.rearrange("(p t) n -> p t n", t=PACK)
         out_scale = sbuf("out_scale", [P, S], U8)
-        for c, (first, width) in enumerate(OUT_CHUNKS):
-            cols = slice(first, first + width)
-            last = c == len(OUT_CHUNKS) - 1
-            z2 = sbuf("z2_%d" % c, [P, PACK, width], F32)
-            for t in range(PACK):
-                nc.vector.tensor_copy(z2[:, t, :], h_gain[t][:].indirect(offsets(mv_sb, first, width)))
-            z2_grouped = sbuf("z2_grouped%d" % c, [P, width, PACK], BF16)
-            interleave(nc.scalar.copy, z2_grouped[:], z2[:])
-            z2_codes = sbuf("z2_codes%d" % c, [P, width], U32)
-            z2_scale = sbuf("z2_scale%d" % c, [P, width], U8)
-            nc.vector.quantize_mx(
-                out=z2_codes[:].bitcast(FP8X4), scales=z2_scale[:], in_=z2_grouped[:].rearrange("p c t -> p (c t)")
-            )
-            acc = bank(c, "out_acc%d" % c, [P, PACK, width])
-            for t in range(PACK):
-                nc.tensor.matmul_mx(
-                    out=acc[:, t, :],
-                    lhsT=w_codes[2][:, t * P : (t + 1) * P].bitcast(FP8X4),
-                    lhsT_scale=w23_scale[4:P, t * P : (t + 1) * P],
-                    rhs=z2_codes[:].bitcast(FP8X4),
-                    rhs_scale=z2_scale[:],
-                    start=True,
-                    stop=True,
+        for half, (first, width) in enumerate(halves):
+            z2 = sbuf("z2_%d" % half, [P, PACK, HALF], F32, "gain_last" if half else "")
+            for t in range(PACK - 1):
+                row = gain_last[:] if half == 0 and t == PACK - 2 else gain_rows[:, t, :]
+                nc.vector.tensor_tensor(
+                    z2[:, t, :], h[t][:].indirect(offsets(mv_sb, first, width)), row, ALU.mult
                 )
-            result = sbuf("result%d" % c, [P, PACK, width], F32)
-            nc.vector.tensor_tensor(result[:], acc[:], res_sb[:, :, cols], ALU.add)
-            nc.sync.dma_start(out=out_rows[:, :, cols], in_=result[:])
-            out_grouped = sbuf("out_grouped%d" % c, [P, width, PACK], BF16)
-            interleave(nc.vector.tensor_copy if last else nc.scalar.copy, out_grouped[:], result[:])
-            out_codes = sbuf("out_codes%d" % c, [P, width], I32)
+            sig = sbuf("sig%d" % half, [P, HALF], F32)
+            nc.scalar.activation(out=sig[:], in_=h[PACK - 1][:].indirect(offsets(mv_sb, first, width)), func=ACT.Sigmoid)
+            nc.vector.tensor_scalar(z2[:, PACK - 1, :], sig[:], affine[:, 0:1], affine[:, 1:2], ALU.mult, ALU.add)
+            z2_grouped = sbuf("z2_grouped%d" % half, [P, HALF, PACK], BF16)
+            on_vector = SPLIT if half == 1 else 0
+            if on_vector:
+                interleave(nc.vector.tensor_copy, z2_grouped[:, :on_vector, :], z2[:, :, :on_vector])
+            interleave(nc.scalar.copy, z2_grouped[:, on_vector:, :], z2[:, :, on_vector:])
+            z2_codes, z2_scale = quantise("z2_%d" % half, z2_grouped)
+            out_grouped = sbuf("out_grouped%d" % half, [P, HALF, PACK], BF16)
+            for part in range(2):
+                inner = slice(part * P, (part + 1) * P)
+                cols = slice(first + part * P, first + (part + 1) * P)
+                acc = bank(2 * half + part, "out_acc%d_%d" % (half, part), [P, PACK, P])
+                for t in range(PACK):
+                    nc.tensor.matmul_mx(
+                        out=acc[:, t, :],
+                        lhsT=w3_codes[:, t * P : (t + 1) * P].bitcast(FP8X4),
+                        lhsT_scale=w23_scale[4:P, t * P : (t + 1) * P],
+                        rhs=z2_codes[:, inner].bitcast(FP8X4),
+                        rhs_scale=z2_scale[:, inner],
+                        start=True,
+                        stop=True,
+                    )
+                result = sbuf("result%d_%d" % (half, part), [P, PACK, P], F32)
+                nc.vector.tensor_tensor(result[:], acc[:], res_sb[:, :, cols], ALU.add)
+                nc.sync.dma_start(out=out_rows[:, :, cols], in_=result[:])
+                last = half == 1 and part == 1
+                interleave(nc.vector.tensor_copy if last else nc.scalar.copy, out_grouped[:, inner, :], result[:])
+            cols = slice(first, first + width)
+            out_codes = sbuf("out_codes%d" % half, [P, HALF], I32)
             nc.vector.quantize_mx(
                 out=out_codes[:].bitcast(FP8X4),
                 scales=out_scale[:, cols],

from contextlib import ExitStack

import concourse.mybir as mybir

K, T, S, N, H = 512, 2048, 512, 512, 512
FLOPS = 2 * S * (K * H + H * H + H * N)

F32 = mybir.dt.float32
BF16 = mybir.dt.bfloat16
I32 = mybir.dt.int32
U32 = mybir.dt.uint32
U16 = mybir.dt.uint16
U8 = mybir.dt.uint8
FP8X4 = mybir.dt.float8_e4m3fn_x4
ALU = mybir.AluOpType
ACT = mybir.ActivationFunctionType

P = 128
PACK = 4
HALF = S // 2
SPLIT = 160


def words_view(words):
    return words[0].rearrange("p c r -> p (c r)").bitcast(I32)


def load_scale_rows(queues, tile, scales, first_row):
    for q in range(4):
        queues[q].dma_start(
            out=tile[32 * q + first_row : 32 * q + first_row + 4, :].bitcast(I32),
            in_=scales[0, 4 * q : 4 * q + 4, :].bitcast(I32),
        )


def deal(engine, dealt, raw, first, end):
    engine.tensor_copy(
        out=dealt[:].rearrange("p (t m) -> p t m", t=PACK)[:, first:end, :],
        in_=raw[:].rearrange("p (m t) -> p t m", t=PACK)[:, first:end, :],
    )


def interleave(copy, grouped, planes):
    copy(
        out=grouped.rearrange("p (c i) t -> p c t i", i=4),
        in_=planes.rearrange("p t (c i) -> p c t i", i=4),
    )


def offsets(lists, first, width):
    return lists[:, first // 16 : (first + width) // 16]


def tile_picked_alldbl3_none_po_kernel(
    tc, x_words, x_scales, w1_words, w1_scales, gn, w2_words, w2_scales, res, w3_words, w3_scales,
    offs, nx, mv, out_0, out_1, out_2,
):
    nc = tc.nc
    with ExitStack() as ctx:
        sb = ctx.enter_context(tc.tile_pool(name="sb", bufs=1))
        psum = ctx.enter_context(tc.psum_pool(name="psum", bufs=1))

        def sbuf(name, shape, dtype, tag=""):
            return sb.tile(shape, dtype, name=name, align_bytes=64, tag=tag or name)

        def bank(number, name, shape):
            return psum.tile(shape, F32, name=name, tag="bank%d" % number)

        offs_sb = sbuf("offs_sb", [P, S // 16], U16)
        nx_sb = sbuf("nx_sb", [P, S // 16], U16)
        mv_sb = sbuf("mv_sb", [P, S // 16], U16)
        x_table = sbuf("x_table", [P, T], I32, "big_load")
        x_scale_table = sbuf("x_scale_table", [P, T], U8, "scale_table")
        w1_raw = sbuf("w1_raw", [P, H], I32, "w_load")
        w1_codes = sbuf("w1_codes", [P, H], I32)
        w1_scale_raw = sbuf("w1_scale_raw", [P, H], U8, "scale_load")
        w1_scale = sbuf("w1_scale", [P, H], U8)
        gain = sbuf("gain", [P, PACK], F32)

        nc.sync.dma_start(offs_sb[:], offs)
        nc.sync.dma_start(nx_sb[:], nx)
        nc.sync.dma_start(mv_sb[:], mv)
        nc.sync.dma_start(out=w1_raw[:], in_=words_view(w1_words))
        nc.sync.dma_start(out=x_table[:], in_=words_view(x_words))
        nc.gpsimd.memset(w1_scale_raw[:].bitcast(I32), 0)
        load_scale_rows([nc.scalar] * 4, w1_scale_raw, w1_scales, 0)
        nc.gpsimd.memset(x_scale_table[:].bitcast(I32), 0)
        load_scale_rows([nc.scalar] * 4, x_scale_table, x_scales, 0)
        nc.gpsimd.dma_start(out=gain[:], in_=gn.rearrange("(p t) o -> p (t o)", t=PACK))

        gain_rows = sbuf("gain_rows", [P, PACK - 1, HALF], F32)
        nc.gpsimd.tensor_copy(gain_rows[:], gain[:, : PACK - 1].unsqueeze(2).to_broadcast([P, PACK - 1, HALF]))
        gain_last = sbuf("gain_last", [P, HALF], F32)
        nc.gpsimd.tensor_copy(gain_last[:], gain[:, PACK - 2 : PACK - 1].to_broadcast([P, HALF]))
        affine = sbuf("affine", [P, 2], F32)
        nc.gpsimd.tensor_scalar(affine[:, 0:1], gain[:, PACK - 1 :], 2.0, 0.0, ALU.mult, ALU.add)
        nc.gpsimd.tensor_scalar(affine[:, 1:2], gain[:, PACK - 1 :], -1.0, 0.0, ALU.mult, ALU.add)

        x_scale = sbuf("x_scale", [P, S], U8, "picked_scale")
        x_codes = sbuf("x_codes", [P, S], U32, "picked_codes")
        deal(nc.vector, w1_codes, w1_raw, 0, PACK)
        nc.vector.tensor_copy(x_codes[:], x_table[:].bitcast(U32).indirect(offs_sb[:]))
        deal(nc.vector, w1_scale, w1_scale_raw, 0, PACK)
        for half in range(2):
            nc.vector.tensor_copy(
                x_scale[:, half * HALF : (half + 1) * HALF],
                x_scale_table[:].indirect(offsets(offs_sb, half * HALF, HALF)),
            )
        w2_raw = sbuf("w2_raw", [P, H], I32, "w_load")
        nc.sync.dma_start(out=w2_raw[:], in_=words_view(w2_words))
        w2_codes = sbuf("w2_codes", [P, H], I32, "scale_table")
        deal(nc.vector, w2_codes, w2_raw, 0, PACK)
        w23_scale_raw = sbuf("w23_scale_raw", [P, H], U8, "scale_load")
        nc.gpsimd.memset(w23_scale_raw[:].bitcast(I32), 0)
        load_scale_rows([nc.sync] * 4, w23_scale_raw, w2_scales, 0)
        load_scale_rows([nc.sync] * 4, w23_scale_raw, w3_scales, 4)
        res_sb = sbuf("res_sb", [P, PACK, S], F32, "big_load")
        nc.sync.dma_start(out=res_sb[:], in_=res.rearrange("(p t) n -> p t n", t=PACK))

        halves = ((0, HALF), (HALF, HALF))

        def windows_and_twins(name):
            wins = [sbuf("%s_win%d" % (name, t), [P, S if t == 0 else 2 * S], F32) for t in range(PACK)]
            last_twin = sbuf("%s_last_twin" % name, [P, S], F32, "%s_twin" % name)
            return wins, [wins[t + 1][:, S:] for t in range(PACK - 1)] + [last_twin[:]]

        y_win, y_twin = windows_and_twins("y")
        p_win, p_twin = windows_and_twins("p")
        for t in range(PACK):
            pieces = halves if t == 0 else ((0, S),)
            for first, width in pieces:
                cols = slice(first, first + width)
                acc = bank(2 * t + first // HALF, "y_acc%d_%d" % (t, first), [P, width])
                nc.tensor.matmul_mx(
                    out=acc[:],
                    lhsT=w1_codes[:, t * P : (t + 1) * P].bitcast(FP8X4),
                    lhsT_scale=w1_scale[:, t * P : (t + 1) * P],
                    rhs=x_codes[:, cols].bitcast(FP8X4),
                    rhs_scale=x_scale[:, cols],
                    start=True,
                    stop=True,
                )
                nc.scalar.copy(out=y_win[t][:, cols], in_=acc[:])
                nc.scalar.copy(out=y_twin[t][:, cols], in_=acc[:])
            for first, width in pieces:
                cols = slice(first, first + width)
                nc.vector.tensor_tensor(
                    p_win[t][:, cols], y_win[t][:].indirect(offsets(nx_sb, first, width)), y_twin[t][:, cols], ALU.add
                )
        for t in range(PACK):
            nc.scalar.copy(out=p_twin[t], in_=p_win[t][:, :S])

        w23_scale = sbuf("w23_scale", [P, H], U8, "y_twin")
        deal(nc.vector, w23_scale, w23_scale_raw, 0, PACK)
        step = [sbuf("step%d" % t, [P, S], F32) for t in range(PACK)]
        rise = [sbuf("rise%d" % t, [P, S], F32) for t in range(PACK)]
        fall = [[sbuf("fall%d_%d" % (t, half), [P, HALF], F32) for half in range(2)] for t in range(PACK)]
        for t in range(PACK):
            for first, width in halves if t == 0 else ((0, S),):
                cols = slice(first, first + width)
                nc.vector.tensor_tensor(
                    step[t][:, cols],
                    p_win[t][:].indirect(offsets(nx_sb, first, width)),
                    p_twin[t][:, cols],
                    ALU.subtract,
                )
            nc.scalar.activation(out=rise[t][:], in_=step[t][:], func=ACT.Relu)
            for half, (first, width) in enumerate(halves):
                nc.scalar.activation(
                    out=fall[t][half][:], in_=step[t][:, first : first + width], func=ACT.Relu, scale=-1.0
                )

        def quantise(name, grouped):
            codes = sbuf(name + "_codes", [P, HALF], U32)
            scale = sbuf(name + "_scale", [P, HALF], U8)
            nc.vector.quantize_mx(
                out=codes[:].bitcast(FP8X4), scales=scale[:], in_=grouped[:].rearrange("p c t -> p (c t)")
            )
            return codes, scale

        h_acc = [[bank(2 * t + half, "h_acc%d_%d" % (t, half), [P, HALF]) for half in range(2)] for t in range(PACK)]
        h = [sbuf("h%d" % t, [P, S], F32) for t in range(PACK)]
        for half, (first, width) in enumerate(halves):
            diff = sbuf("diff%d" % half, [P, PACK, HALF], F32, "fall3_0" if half else "p_win3")
            z_grouped = sbuf("z_grouped%d" % half, [P, HALF, PACK], BF16, "z_grouped")
            for t in range(PACK):
                nc.vector.tensor_tensor(
                    diff[:, t, :], rise[t][:].indirect(offsets(nx_sb, first, width)), fall[t][half][:], ALU.subtract
                )
            if half == 0:
                z = sbuf("z", [P, PACK, HALF], F32)
                for t in range(PACK):
                    nc.scalar.activation(out=z[:, t, :], in_=diff[:, t, :], func=ACT.Copy, scale=gain[:, t : t + 1])
                interleave(nc.scalar.copy, z_grouped[:], z[:])
            else:
                nc.vector.tensor_tensor(
                    z_grouped[:].rearrange("p (c i) t -> p c t i", i=4),
                    diff[:].rearrange("p t (c i) -> p c t i", i=4),
                    gain[:].unsqueeze(1).unsqueeze(3).to_broadcast([P, HALF // 4, PACK, 4]),
                    ALU.mult,
                )
            z_codes, z_scale = quantise("z%d" % half, z_grouped)
            for t in range(PACK):
                nc.tensor.matmul_mx(
                    out=h_acc[t][half][:],
                    lhsT=w2_codes[:, t * P : (t + 1) * P].bitcast(FP8X4),
                    lhsT_scale=w23_scale[:, t * P : (t + 1) * P],
                    rhs=z_codes[:].bitcast(FP8X4),
                    rhs_scale=z_scale[:],
                    start=True,
                    stop=True,
                )
        w3_raw = sbuf("w3_raw", [P, H], I32, "w_load")
        nc.sync.dma_start(out=w3_raw[:], in_=words_view(w3_words))
        w3_codes = sbuf("w3_codes", [P, H], I32, "p_twin")
        deal(nc.vector, w3_codes, w3_raw, 0, PACK)
        for t in range(PACK):
            for half, (first, width) in enumerate(halves):
                if t < PACK - 1:
                    nc.scalar.activation(
                        out=h[t][:, first : first + width], in_=h_acc[t][half][:], func=ACT.Tanh, scale=-1.0
                    )
                else:
                    nc.scalar.activation(
                        out=h[t][:, first : first + width], in_=h_acc[t][half][:], func=ACT.Copy, scale=-2.0
                    )

        out_rows = out_0.rearrange("(p t) n -> p t n", t=PACK)
        out_scale = sbuf("out_scale", [P, S], U8)
        for half, (first, width) in enumerate(halves):
            z2 = sbuf("z2_%d" % half, [P, PACK, HALF], F32, "gain_last" if half else "")
            for t in range(PACK - 1):
                row = gain_last[:] if half == 0 and t == PACK - 2 else gain_rows[:, t, :]
                nc.vector.tensor_tensor(
                    z2[:, t, :], h[t][:].indirect(offsets(mv_sb, first, width)), row, ALU.mult
                )
            sig = sbuf("sig%d" % half, [P, HALF], F32)
            nc.scalar.activation(out=sig[:], in_=h[PACK - 1][:].indirect(offsets(mv_sb, first, width)), func=ACT.Sigmoid)
            nc.vector.tensor_scalar(z2[:, PACK - 1, :], sig[:], affine[:, 0:1], affine[:, 1:2], ALU.mult, ALU.add)
            z2_grouped = sbuf("z2_grouped%d" % half, [P, HALF, PACK], BF16)
            on_vector = SPLIT if half == 1 else 0
            if on_vector:
                interleave(nc.vector.tensor_copy, z2_grouped[:, :on_vector, :], z2[:, :, :on_vector])
            interleave(nc.scalar.copy, z2_grouped[:, on_vector:, :], z2[:, :, on_vector:])
            z2_codes, z2_scale = quantise("z2_%d" % half, z2_grouped)
            out_grouped = sbuf("out_grouped%d" % half, [P, HALF, PACK], BF16)
            for part in range(2):
                inner = slice(part * P, (part + 1) * P)
                cols = slice(first + part * P, first + (part + 1) * P)
                acc = bank(2 * half + part, "out_acc%d_%d" % (half, part), [P, PACK, P])
                for t in range(PACK):
                    nc.tensor.matmul_mx(
                        out=acc[:, t, :],
                        lhsT=w3_codes[:, t * P : (t + 1) * P].bitcast(FP8X4),
                        lhsT_scale=w23_scale[4:P, t * P : (t + 1) * P],
                        rhs=z2_codes[:, inner].bitcast(FP8X4),
                        rhs_scale=z2_scale[:, inner],
                        start=True,
                        stop=True,
                    )
                result = sbuf("result%d_%d" % (half, part), [P, PACK, P], F32)
                nc.vector.tensor_tensor(result[:], acc[:], res_sb[:, :, cols], ALU.add)
                nc.sync.dma_start(out=out_rows[:, :, cols], in_=result[:])
                last = half == 1 and part == 1
                interleave(nc.vector.tensor_copy if last else nc.scalar.copy, out_grouped[:, inner, :], result[:])
            cols = slice(first, first + width)
            out_codes = sbuf("out_codes%d" % half, [P, HALF], I32)
            nc.vector.quantize_mx(
                out=out_codes[:].bitcast(FP8X4),
                scales=out_scale[:, cols],
                in_=out_grouped[:].rearrange("p c t -> p (c t)"),
            )
            nc.sync.dma_start(out=words_view(out_1)[:, cols], in_=out_codes[:])
        for q in range(4):
            queue = nc.scalar if q % 2 else nc.sync
            queue.dma_start(
                out=out_2[0, 4 * q : 4 * q + 4, :].bitcast(I32),
                in_=out_scale[32 * q : 32 * q + 4, :].bitcast(I32),
            )
